import numpy as np
import ml_dtypes

BF16 = ml_dtypes.bfloat16


def bf(x):
    return np.asarray(x, np.float32).astype(BF16)


def f32(x):
    return np.asarray(x, np.float32)


def f64(x):
    return np.asarray(x).astype(np.float64)


def striped(idx):
    return np.concatenate([l.reshape(-1, 16).T for l in idx])


def rows(idx, k):
    return np.tile(np.repeat(idx, 16, axis=0), (k // (16 * 8), 1))


def look(tab, idx):
    return np.take_along_axis(f64(tab), rows(idx, len(tab)), axis=1)


K, S, V, N = 256, 2048, 1024, 1024


def setup_inputs():
    return {"tab": f32(np.random.standard_normal((2, K, S))), "y": f32(np.random.standard_normal((K, V))), "offs": striped(np.stack([np.random.permutation(S)[:N] for _ in range(8)]))}


def reference(tab, y, offs):
    idx = np.stack([g.T.reshape(-1) for g in np.split(offs, 8)])
    x = (np.minimum(look(tab[0], idx), f64(y))) * (np.maximum(look(tab[1], idx), 0.0))
    return x

@@ -1,0 +1,44 @@
+import concourse.mybir as mybir
+
+F32, U16 = mybir.dt.float32, mybir.dt.uint16
+MIN, MULT = mybir.AluOpType.min, mybir.AluOpType.mult
+RELU = mybir.ActivationFunctionType.Relu
+
+P = 128
+ROWS = 256
+PLACES = 2048
+N = 1024
+PIECE = 512
+FLOPS = 3 * ROWS * N
+
+
+def tile_lookup_vg_minrelu_out_kernel(tc, tab, y, offs, out):
+    nc = tc.nc
+    with (
+        tc.tile_pool(name="lists", bufs=1) as lists,
+        tc.tile_pool(name="windows", bufs=2) as windows,
+        tc.tile_pool(name="streams", bufs=2) as streams,
+        tc.tile_pool(name="pieces", bufs=4) as pieces,
+    ):
+        offsets = lists.tile([P, N // 16], U16)
+        nc.sync.dma_start(offsets[:], offs)
+
+        for block in range(ROWS // P):
+            rows = slice(block * P, (block + 1) * P)
+            values = windows.tile([P, PLACES], F32)
+            stream = streams.tile([P, N], F32)
+            gates = windows.tile([P, PLACES], F32)
+            nc.sync.dma_start(values[:], tab[0, rows, :])
+            nc.sync.dma_start(stream[:], y[rows, :])
+            nc.sync.dma_start(gates[:], tab[1, rows, :])
+
+            for start in range(0, N, PIECE):
+                cols = slice(start, start + PIECE)
+                picks = offsets[:, start // 16 : (start + PIECE) // 16]
+                capped = pieces.tile([P, PIECE], F32)
+                gate = pieces.tile([P, PIECE], F32)
+                product = pieces.tile([P, PIECE], F32)
+                nc.vector.tensor_tensor(capped[:], values[:].indirect(picks), stream[:, cols], MIN)
+                nc.scalar.activation(gate[:], gates[:].indirect(picks), RELU)
+                nc.vector.tensor_tensor(product[:], capped[:], gate[:], MULT)
+                nc.sync.dma_start(out[rows, cols], product[:])

@@ -14,31 +14,33 @@ FLOPS = 3 * ROWS * N
 
 def tile_lookup_vg_minrelu_out_kernel(tc, tab, y, offs, out):
     nc = tc.nc
+    blocks = [slice(start, start + P) for start in range(0, ROWS, P)]
     with (
         tc.tile_pool(name="lists", bufs=1) as lists,
-        tc.tile_pool(name="windows", bufs=2) as windows,
-        tc.tile_pool(name="streams", bufs=2) as streams,
+        tc.tile_pool(name="inputs", bufs=1) as inputs,
         tc.tile_pool(name="pieces", bufs=4) as pieces,
     ):
         offsets = lists.tile([P, N // 16], U16)
         nc.sync.dma_start(offsets[:], offs)
+        values, streams, gates = [], [], []
+        for b, rows in enumerate(blocks):
+            values.append(inputs.tile([P, PLACES], F32, name=f"values{b}"))
+            streams.append(inputs.tile([P, N], F32, name=f"stream{b}"))
+            gates.append(inputs.tile([P, PLACES], F32, name=f"gates{b}"))
+            nc.sync.dma_start(values[b][:], tab[0, rows, :])
+            early = N - PIECE if b == len(blocks) - 1 else N
+            nc.sync.dma_start(streams[b][:, 0:early], y[rows, 0:early])
+            nc.sync.dma_start(gates[b][:], tab[1, rows, :])
+        nc.sync.dma_start(streams[-1][:, N - PIECE : N], y[blocks[-1], N - PIECE : N])
 
-        for block in range(ROWS // P):
-            rows = slice(block * P, (block + 1) * P)
-            values = windows.tile([P, PLACES], F32)
-            stream = streams.tile([P, N], F32)
-            gates = windows.tile([P, PLACES], F32)
-            nc.sync.dma_start(values[:], tab[0, rows, :])
-            nc.sync.dma_start(stream[:], y[rows, :])
-            nc.sync.dma_start(gates[:], tab[1, rows, :])
-
+        for b, rows in enumerate(blocks):
             for start in range(0, N, PIECE):
                 cols = slice(start, start + PIECE)
                 picks = offsets[:, start // 16 : (start + PIECE) // 16]
                 capped = pieces.tile([P, PIECE], F32)
                 gate = pieces.tile([P, PIECE], F32)
                 product = pieces.tile([P, PIECE], F32)
-                nc.vector.tensor_tensor(capped[:], values[:].indirect(picks), stream[:, cols], MIN)
-                nc.scalar.activation(gate[:], gates[:].indirect(picks), RELU)
+                nc.vector.tensor_tensor(capped[:], values[b][:].indirect(picks), streams[b][:, cols], MIN)
+                nc.scalar.activation(gate[:], gates[b][:].indirect(picks), RELU)
                 nc.vector.tensor_tensor(product[:], capped[:], gate[:], MULT)
                 nc.sync.dma_start(out[rows, cols], product[:])

@@ -9,6 +9,7 @@ ROWS = 256
 PLACES = 2048
 N = 1024
 PIECE = 512
+HALF = PIECE // 2
 FLOPS = 3 * ROWS * N
 
 
@@ -39,8 +40,10 @@ def tile_lookup_vg_minrelu_out_kernel(tc, tab, y, offs, out):
                 picks = offsets[:, start // 16 : (start + PIECE) // 16]
                 capped = pieces.tile([P, PIECE], F32)
                 gate = pieces.tile([P, PIECE], F32)
-                product = pieces.tile([P, PIECE], F32)
                 nc.vector.tensor_tensor(capped[:], values[b][:].indirect(picks), streams[b][:, cols], MIN)
                 nc.scalar.activation(gate[:], gates[b][:].indirect(picks), RELU)
-                nc.vector.tensor_tensor(product[:], capped[:], gate[:], MULT)
-                nc.sync.dma_start(out[rows, cols], product[:])
+                for at in range(0, PIECE, HALF):
+                    part = slice(at, at + HALF)
+                    product = pieces.tile([P, HALF], F32)
+                    nc.vector.tensor_tensor(product[:], capped[:, part], gate[:, part], MULT)
+                    nc.sync.dma_start(out[rows, start + at : start + at + HALF], product[:])

import concourse.mybir as mybir

F32, U16 = mybir.dt.float32, mybir.dt.uint16
MIN, MULT = mybir.AluOpType.min, mybir.AluOpType.mult
RELU = mybir.ActivationFunctionType.Relu

P = 128
ROWS = 256
PLACES = 2048
N = 1024
PIECE = 512
HALF = PIECE // 2
FLOPS = 3 * ROWS * N


def tile_lookup_vg_minrelu_out_kernel(tc, tab, y, offs, out):
    nc = tc.nc
    blocks = [slice(start, start + P) for start in range(0, ROWS, P)]
    with (
        tc.tile_pool(name="lists", bufs=1) as lists,
        tc.tile_pool(name="inputs", bufs=1) as inputs,
        tc.tile_pool(name="pieces", bufs=4) as pieces,
    ):
        offsets = lists.tile([P, N // 16], U16)
        nc.sync.dma_start(offsets[:], offs)
        values, streams, gates = [], [], []
        for b, rows in enumerate(blocks):
            values.append(inputs.tile([P, PLACES], F32, name=f"values{b}"))
            streams.append(inputs.tile([P, N], F32, name=f"stream{b}"))
            gates.append(inputs.tile([P, PLACES], F32, name=f"gates{b}"))
            nc.sync.dma_start(values[b][:], tab[0, rows, :])
            early = N - PIECE if b == len(blocks) - 1 else N
            nc.sync.dma_start(streams[b][:, 0:early], y[rows, 0:early])
            nc.sync.dma_start(gates[b][:], tab[1, rows, :])
        nc.sync.dma_start(streams[-1][:, N - PIECE : N], y[blocks[-1], N - PIECE : N])

        for b, rows in enumerate(blocks):
            for start in range(0, N, PIECE):
                cols = slice(start, start + PIECE)
                picks = offsets[:, start // 16 : (start + PIECE) // 16]
                capped = pieces.tile([P, PIECE], F32)
                gate = pieces.tile([P, PIECE], F32)
                nc.vector.tensor_tensor(capped[:], values[b][:].indirect(picks), streams[b][:, cols], MIN)
                nc.scalar.activation(gate[:], gates[b][:].indirect(picks), RELU)
                for at in range(0, PIECE, HALF):
                    part = slice(at, at + HALF)
                    product = pieces.tile([P, HALF], F32)
                    nc.vector.tensor_tensor(product[:], capped[:, part], gate[:, part], MULT)
                    nc.sync.dma_start(out[rows, start + at : start + at + HALF], product[:])
